import numpy as np
import ml_dtypes


def mxq(x, axis, fmt="e4m3"):
    dtype, down = {"e4m3": (ml_dtypes.float8_e4m3fn, 7), "e5m2": (ml_dtypes.float8_e5m2, 14)}[fmt]
    v = np.moveaxis(np.asarray(x, np.float32).astype(ml_dtypes.bfloat16).astype(np.float64), axis, -1)
    blocks = v.reshape(v.shape[:-1] + (-1, 32))
    amax = np.abs(blocks).max(-1, keepdims=True)
    byte = np.maximum(np.where(amax > 0, np.frexp(amax)[1] - 1 + 127, 0) - down, 1)
    scale = np.exp2(byte - 127.0)
    codes = (blocks / scale).astype(np.float32).astype(dtype).astype(np.float64)
    return np.moveaxis((codes * scale).reshape(v.shape), -1, axis)


WIDE = False


def mx_kscale(k):
    if not WIDE:
        return np.ones(k)
    levels = np.array([30, -30])
    if k % 512:
        return np.exp2(np.random.permutation(np.resize(levels, k // 32))).repeat(32)
    a = np.empty((k // 512, 16))
    for p in range(k // 512):
        a[p, :8] = np.random.permutation(np.resize(levels, 8))
        for g in range(8):
            far = levels[np.abs(levels - a[p, g]) >= 10]
            a[p, g + 8] = far[np.random.randint(len(far))]
    return np.exp2(a.ravel()).repeat(32)


def f64(x):
    return np.asarray(x).astype(np.float64)


def striped(idx):
    return np.tile(np.asarray(idx).reshape(-1, 16).T, (8, 1)).astype(np.uint16)


def unstriped(offs):
    return offs[:16].T.reshape(-1).astype(np.int64)


E2M1 = np.array([0.0, 0.5, 1.0, 1.5, 2.0, 3.0, 4.0, 6.0, -0.0, -0.5, -1.0, -1.5, -2.0, -3.0, -4.0, -6.0])


def pack_weight(w, fmt):
    k, n = w.shape
    w = f64(np.asarray(w, np.float32).astype(ml_dtypes.bfloat16)).reshape(k // 32, 32, n)
    amax = np.abs(w).max(1)
    if fmt == "e4m3":
        byte = np.frexp(amax)[1] - 1 + 127 - 7
    else:
        mant, ex = np.frexp(amax / 6.0)
        byte = np.where(mant > 0.5, ex, ex - 1) + 127
    byte = np.clip(np.where(amax > 0, byte, 1), 1, 254)
    scaled = (w * np.exp2(127.0 - byte)[:, None, :]).reshape(k, n).astype(np.float32)
    by_word = np.ascontiguousarray(scaled.reshape(k // 512, 128, 4, n).transpose(0, 1, 3, 2))
    if fmt == "e4m3":
        words = by_word.astype(ml_dtypes.float8_e4m3fn).view(np.uint8)
    else:
        c = by_word.astype(ml_dtypes.float4_e2m1fn).view(np.uint8) & 0xF
        words = (c[..., 0::2] | (c[..., 1::2] << 4)).reshape(k // 512, 128, 2 * n)
    return np.ascontiguousarray(words), np.ascontiguousarray(byte.astype(np.uint8).reshape(k // 512, 16, n))


def unpack_weight(words, scales, fmt):
    g, _, n = scales.shape
    words = np.ascontiguousarray(words).reshape(g, 128, n, -1)
    if fmt == "e4m3":
        vals = words.view(ml_dtypes.float8_e4m3fn).astype(np.float64)
    else:
        nib = np.empty((g, 128, n, 4), np.uint8)
        nib[..., 0::2] = words & 0xF
        nib[..., 1::2] = words >> 4
        vals = E2M1[nib]
    vals = vals * np.repeat(np.exp2(scales.astype(np.float64) - 127.0), 8, axis=1)[..., None]
    return vals.transpose(0, 1, 3, 2).reshape(g * 512, n)


def bf(x):
    return np.asarray(x, np.float32).astype(ml_dtypes.bfloat16)


def planes(Y):
    r, m = Y.shape
    b = f64(bf(Y)).reshape(r // 32, 32, m)
    amax = np.abs(b).max(1)
    byte = np.clip(np.where(amax > 0, np.frexp(amax)[1] - 1 + 127 - 7, 1), 1, 254)
    codes = (b * np.exp2(127.0 - byte)[:, None, :]).reshape(r, m).astype(np.float32).astype(ml_dtypes.float8_e4m3fn).view(np.uint8)
    words = codes.reshape(r // 512, 128, 4, m).transpose(0, 1, 3, 2)
    return np.ascontiguousarray(words), np.ascontiguousarray(byte.astype(np.uint8).reshape(r // 512, 16, m))


N, R, K, J, I = 1024, 512, 512, 1024, 512


def setup_inputs():
    n = np.random.standard_normal
    idx = np.random.permutation(J)[:I]
    fn = mx_kscale(N)
    fr = mx_kscale(R)
    gp = pack_weight(n((N, I)) / fn[:, None], "e2m1")
    wdp = pack_weight(n((N, R)) * 1 / np.sqrt(N) * fn[:, None], "e4m3")
    wup = pack_weight(n((R, K)) * 1 / np.sqrt(R) / fr[:, None], "e2m1")
    return {
        "g_words": gp[0],
        "g_scales": gp[1],
        "wd_words": wdp[0],
        "wd_scales": wdp[1],
        "z": (n((R, J)) * fr[:, None]).astype(np.float32),
        "wu_words": wup[0],
        "wu_scales": wup[1],
        "run": (0.5 * n((K, J))).astype(np.float32),
        "offs": striped(idx),
    }


def reference(g_words, g_scales, wd_words, wd_scales, z, wu_words, wu_scales, run, offs):
    idx = unstriped(offs)
    gu = unpack_weight(g_words, g_scales, "e2m1")
    wdu = unpack_weight(wd_words, wd_scales, "e4m3")
    wuu = unpack_weight(wu_words, wu_scales, "e2m1")
    d = wdu.T @ gu
    dp = np.zeros((R, J))
    dp[:, idx] = d
    dz = 2.0 * dp * np.maximum(f64(z), 0.0)
    dzq = mxq(dz, 0, "e5m2")
    p = wuu.T @ dzq
    y = p + f64(run)
    words, scales = planes(y)
    return y, words, scales

@@ -1,0 +1,221 @@
+from contextlib import ExitStack
+
+import concourse.mybir as mybir
+
+N, R, K, J, I = 1024, 512, 512, 1024, 512
+FLOPS = 2 * N * R * I + 2 * R * K * J
+
+F32 = mybir.dt.float32
+BF16 = mybir.dt.bfloat16
+I32 = mybir.dt.int32
+U16 = mybir.dt.uint16
+U8 = mybir.dt.uint8
+E4M3 = mybir.dt.float8_e4m3fn_x4
+E5M2 = mybir.dt.float8_e5m2_x4
+E2M1 = mybir.dt.float4_e2m1fn_x4
+MULT = mybir.AluOpType.mult
+ADD = mybir.AluOpType.add
+RELU = mybir.ActivationFunctionType.Relu
+
+P = 128
+PACK = 4
+PASSES = N // (P * PACK)
+HALF = 512
+QUARTER = 256
+FIRST = 128
+
+
+def tile_list_listed_slots_back_through_rest_pl_kernel(
+    tc, g_words, g_scales, wd_words, wd_scales, z, wu_words, wu_scales, run, offs, out_0, out_1, out_2
+):
+    nc = tc.nc
+    with ExitStack() as ctx:
+        sb = ctx.enter_context(tc.tile_pool(name="sb", bufs=1))
+        ps = ctx.enter_context(tc.psum_pool(name="ps", bufs=1))
+
+        def tile(shape, dtype, name, tag=None):
+            return sb.tile(shape, dtype, name=name, tag=tag or name, align_bytes=64)
+
+        def bank(b, name):
+            return ps.tile([P, HALF], F32, name=name, tag="bank%d" % b)
+
+        offsets = tile([P, I // 16], U16, "offsets")
+        wd_raw = tile([P, PASSES, R], I32, "wd_raw", "late_b")
+        wds_raw = tile([P, PASSES, R], U8, "wds_raw", "late_a")
+        g_w = tile([P, PASSES, 2 * I], U8, "g_w")
+        g_s = tile([P, PASSES, I], U8, "g_s")
+
+        nc.vector.memset(wds_raw[:].bitcast(I32), 0)
+        nc.gpsimd.memset(g_s[:].bitcast(I32), 0)
+
+        nc.sync.dma_start(offsets[:], offs)
+        nc.sync.dma_start(wd_raw[:], wd_words.rearrange("z p c r -> p z (c r)").bitcast(I32))
+        nc.scalar.dma_start(g_w[:].bitcast(I32), g_words.rearrange("z p b -> p z b").bitcast(I32))
+        for q in range(4):
+            nc.sync.dma_start(
+                wds_raw[32 * q : 32 * q + 4, :, :].bitcast(I32),
+                wd_scales[:, 4 * q : 4 * q + 4, :].rearrange("z q c -> q z c").bitcast(I32),
+            )
+        for q in range(4):
+            queue = nc.scalar if q < 3 else nc.gpsimd
+            queue.dma_start(
+                g_s[32 * q : 32 * q + 4, :, :].bitcast(I32),
+                g_scales[:, 4 * q : 4 * q + 4, :].rearrange("z q c -> q z c").bitcast(I32),
+            )
+
+        pages = [tile([P, J], F32, "page%d" % t) for t in range(PACK)]
+        nc.vector.memset(pages[0][:], 0.0)
+        nc.gpsimd.memset(pages[1][:], 0.0)
+
+        wu_raw = tile([P, 3 * K], U8, "wu_raw")
+        nc.vector.memset(wu_raw[:].bitcast(I32), 0)
+        nc.sync.dma_start(wu_raw[:, 0 : 2 * K].bitcast(I32), wu_words[0].bitcast(I32))
+        for q in range(4):
+            nc.sync.dma_start(
+                wu_raw[32 * q : 32 * q + 4, 2 * K : 3 * K].bitcast(I32),
+                wu_scales[0, 4 * q : 4 * q + 4, :].bitcast(I32),
+            )
+        wu_d = tile([P, PACK, 2 * P], U8, "wu_d")
+        wus_d = tile([P, PACK, P], U8, "wus_d")
+        nc.gpsimd.tensor_copy(
+            wu_d[:].rearrange("p t (m b) -> p t m b", b=2),
+            wu_raw[:, 0 : 2 * K].rearrange("p (m t b) -> p t m b", t=PACK, b=2),
+        )
+        nc.gpsimd.tensor_copy(wus_d[:], wu_raw[:, 2 * K : 3 * K].rearrange("p (m t) -> p t m", t=PACK))
+
+        for t in range(2, PACK):
+            nc.vector.memset(pages[t][:], 0.0)
+
+        wd0 = tile([P, PASSES, P], I32, "wd0")
+        wds0 = tile([P, PASSES, P], U8, "wds0")
+        wdr = tile([P, PACK - 1, PASSES, P], I32, "wdr")
+        wdsr = tile([P, PACK - 1, PASSES, P], U8, "wdsr")
+        wd_v = wd_raw[:].rearrange("p z (m t) -> p z m t", t=PACK)
+        wds_v = wds_raw[:].rearrange("p z (m t) -> p z m t", t=PACK)
+        nc.vector.tensor_copy(wds0[:], wds_v[:, :, :, 0])
+        nc.vector.tensor_copy(wd0[:], wd_v[:, :, :, 0])
+        nc.vector.tensor_copy(wdr[:].rearrange("p t z m -> p z m t"), wd_v[:, :, :, 1:PACK])
+        nc.vector.tensor_copy(wdsr[:].rearrange("p t z m -> p z m t"), wds_v[:, :, :, 1:PACK])
+
+        def first_product(t, acc, lo, hi):
+            for zp in range(PASSES):
+                w = wd0[:, zp, :] if t == 0 else wdr[:, t - 1, zp, :]
+                s = wds0[:, zp, :] if t == 0 else wdsr[:, t - 1, zp, :]
+                nc.tensor.matmul_mx(
+                    out=acc,
+                    lhsT=w.bitcast(E4M3),
+                    lhsT_scale=s,
+                    rhs=g_w[:, zp, 2 * lo : 2 * hi].bitcast(E2M1),
+                    rhs_scale=g_s[:, zp, lo:hi],
+                    start=(zp == 0),
+                    stop=(zp == PASSES - 1),
+                )
+
+        z_v = z.rearrange("(p t) j -> p t j", t=PACK)
+        z_a = tile([P, 2, J], F32, "z_a", "late_a")
+        z_b = tile([P, 2, J], F32, "z_b", "late_b")
+        nc.sync.dma_start(z_a[:], z_v[:, 0:2, :])
+        nc.sync.dma_start(z_b[:], z_v[:, 2:4, :])
+        z_rows = [z_a[:, 0, :], z_a[:, 1, :], z_b[:, 0, :], z_b[:, 1, :]]
+
+        pairs = [tile([P, 2, 2 * HALF], BF16, "pairs%d" % h) for h in range(2)]
+
+        def multiply(engine, t, h):
+            cols = slice(h * HALF, (h + 1) * HALF)
+            gate = tile([P, HALF], F32, "gate%d_%d" % (t, h), "gate%d_%d" % (min(t, 2), h))
+            nc.scalar.activation(gate[:], z_rows[t][:, cols], RELU, scale=2.0)
+            engine.tensor_tensor(pairs[h][:, t // 2, t % 2 : 2 * HALF : 2], pages[t][:, cols], gate[:], MULT)
+
+        acc = bank(0, "d0a")
+        first_product(0, acc[:, 0:FIRST], 0, FIRST)
+        d0a = tile([P, FIRST], F32, "d0a_s", "late_e")
+        nc.scalar.copy(d0a[:], acc[:, 0:FIRST])
+        nc.vector.tensor_copy(pages[0][:].indirect(offsets[:, 0 : FIRST // 16]), d0a[:])
+        acc = bank(1, "d0b")
+        for lo in range(FIRST, I, FIRST):
+            first_product(0, acc[:, lo - FIRST : lo], lo, lo + FIRST)
+        d0b = tile([P, I - FIRST], F32, "d0b_s", "late_f")
+        nc.scalar.copy(d0b[:], acc[:, 0 : I - FIRST])
+        nc.vector.tensor_copy(pages[0][:].indirect(offsets[:, FIRST // 16 : I // 16]), d0b[:])
+
+        for t in range(1, PACK):
+            acc = bank(t + 1, "d%d" % t)
+            first_product(t, acc[:], 0, I)
+            d_s = tile([P, I], F32, "d%d_s" % t)
+            nc.scalar.copy(d_s[:], acc[:])
+            nc.vector.tensor_copy(pages[t][:].indirect(offsets[:]), d_s[:])
+
+        run_v = run.rearrange("(p t) j -> p t j", t=PACK)
+        runs = [tile([P, PACK, HALF], F32, "run%d" % h, ("late_e", "late_f")[h]) for h in range(2)]
+        for h in range(2):
+            nc.sync.dma_start(runs[h][:], run_v[:, :, h * HALF : (h + 1) * HALF])
+
+        for t in range(PACK - 1):
+            for h in range(2):
+                multiply(nc.gpsimd, t, h)
+        for h in range(2):
+            multiply(nc.vector, PACK - 1, h)
+
+        dz_w = [tile([P, HALF], I32, "dz_w%d" % h) for h in range(2)]
+        dz_s = [tile([P, HALF], U8, "dz_s%d" % h) for h in range(2)]
+        for q in range(4):
+            h, lo = q // 2, (q % 2) * QUARTER
+            grouped = tile([P, PACK * QUARTER], BF16, "dz_g%d" % q)
+            nc.scalar.copy(
+                grouped[:].bitcast(F32).rearrange("p (j u) -> p j u", u=2),
+                pairs[h][:].bitcast(F32)[:, :, lo : lo + QUARTER].rearrange("p u j -> p j u"),
+            )
+            nc.vector.quantize_mx(
+                out=dz_w[h][:, lo : lo + QUARTER].bitcast(E5M2), scales=dz_s[h][:, lo : lo + QUARTER], in_=grouped[:]
+            )
+
+        out_v = out_0.rearrange("(p t) j -> p t j", t=PACK)
+        words_v = out_1[0].rearrange("p c r -> p (c r)").bitcast(I32)
+        y_w = tile([P, J], I32, "y_w")
+        y_s = tile([P, J], U8, "y_s")
+
+        def second_product(h, t):
+            acc = bank((5 + PACK * h + t) % 8, "p%d_%d" % (h, t))
+            nc.tensor.matmul_mx(
+                out=acc[:],
+                lhsT=wu_d[:, t, :].bitcast(E2M1),
+                lhsT_scale=wus_d[:, t, :],
+                rhs=dz_w[h][:].bitcast(E5M2),
+                rhs_scale=dz_s[h][:],
+                start=True,
+                stop=True,
+            )
+            return acc
+
+        def planes(q, y, on_gpsimd):
+            grouped = tile([P, QUARTER, PACK], BF16, "y_g%d" % q)
+            dst = grouped[:].rearrange("p (c i) t -> p c t i", i=4)
+            src = y.rearrange("p t (c i) -> p c t i", i=4)
+            if on_gpsimd:
+                nc.gpsimd.tensor_scalar(grouped[:], y.rearrange("p t j -> p j t"), 1.0, 0.0, MULT, ADD)
+            else:
+                nc.scalar.copy(dst, src)
+            cols = slice(q * QUARTER, (q + 1) * QUARTER)
+            nc.vector.quantize_mx(
+                out=y_w[:, cols].bitcast(E4M3), scales=y_s[:, cols], in_=grouped[:].rearrange("p j t -> p (j t)")
+            )
+            nc.sync.dma_start(words_v[:, cols], y_w[:, cols])
+
+        accs = [[second_product(h, t) for t in range(PACK)] for h in range(2)]
+        y0 = tile([P, PACK, HALF], F32, "y0")
+        for t in range(PACK):
+            nc.vector.tensor_tensor(y0[:, t, :], accs[0][t][:], runs[0][:, t, :], ADD)
+            nc.sync.dma_start(out_v[:, t, 0:HALF], y0[:, t, :])
+        y1 = [tile([P, PACK, QUARTER], F32, "y1_%d" % e) for e in range(2)]
+        for e in range(2):
+            cols = slice(e * QUARTER, (e + 1) * QUARTER)
+            for t in range(PACK):
+                nc.vector.tensor_tensor(y1[e][:, t, :], accs[1][t][:, cols], runs[1][:, t, cols], ADD)
+            nc.sync.dma_start(out_v[:, :, HALF + e * QUARTER : HALF + (e + 1) * QUARTER], y1[e][:])
+        planes(0, y0[:, :, 0:QUARTER], False)
+        planes(1, y0[:, :, QUARTER:HALF], True)
+        planes(2, y1[0][:], False)
+        planes(3, y1[1][:], False)
+        for q in range(4):
+            queue = nc.sync if q % 2 == 0 else nc.scalar
+            queue.dma_start(out_2[0, 4 * q : 4 * q + 4, :].bitcast(I32), y_s[32 * q : 32 * q + 4, :].bitcast(I32))

@@ -42,30 +42,28 @@ def tile_list_listed_slots_back_through_rest_pl_kernel(
         offsets = tile([P, I // 16], U16, "offsets")
         wd_raw = tile([P, PASSES, R], I32, "wd_raw", "late_b")
         wds_raw = tile([P, PASSES, R], U8, "wds_raw", "late_a")
-        g_w = tile([P, PASSES, 2 * I], U8, "g_w")
-        g_s = tile([P, PASSES, I], U8, "g_s")
+        g_w = tile([P, PASSES, 2 * I], U8, "g_w", "late_h")
+        g_s = tile([P, PASSES, I], U8, "g_s", "late_i")
 
         nc.vector.memset(wds_raw[:].bitcast(I32), 0)
-        nc.gpsimd.memset(g_s[:].bitcast(I32), 0)
 
-        nc.sync.dma_start(offsets[:], offs)
-        nc.sync.dma_start(wd_raw[:], wd_words.rearrange("z p c r -> p z (c r)").bitcast(I32))
-        nc.scalar.dma_start(g_w[:].bitcast(I32), g_words.rearrange("z p b -> p z b").bitcast(I32))
+        queues = (nc.sync, nc.scalar)
         for q in range(4):
-            nc.sync.dma_start(
-                wds_raw[32 * q : 32 * q + 4, :, :].bitcast(I32),
-                wd_scales[:, 4 * q : 4 * q + 4, :].rearrange("z q c -> q z c").bitcast(I32),
-            )
-        for q in range(4):
-            queue = nc.scalar if q < 3 else nc.gpsimd
-            queue.dma_start(
+            queues[q % 2].dma_start(
                 g_s[32 * q : 32 * q + 4, :, :].bitcast(I32),
                 g_scales[:, 4 * q : 4 * q + 4, :].rearrange("z q c -> q z c").bitcast(I32),
             )
+        nc.sync.dma_start(wd_raw[:], wd_words.rearrange("z p c r -> p z (c r)").bitcast(I32))
+        nc.scalar.dma_start(g_w[:].bitcast(I32), g_words.rearrange("z p b -> p z b").bitcast(I32))
+        for q in range(4):
+            queues[q % 2].dma_start(
+                wds_raw[32 * q : 32 * q + 4, :, :].bitcast(I32),
+                wd_scales[:, 4 * q : 4 * q + 4, :].rearrange("z q c -> q z c").bitcast(I32),
+            )
+        nc.sync.dma_start(offsets[:], offs)
 
         pages = [tile([P, J], F32, "page%d" % t) for t in range(PACK)]
         nc.vector.memset(pages[0][:], 0.0)
-        nc.gpsimd.memset(pages[1][:], 0.0)
 
         wu_raw = tile([P, 3 * K], U8, "wu_raw")
         nc.vector.memset(wu_raw[:].bitcast(I32), 0)
@@ -75,56 +73,43 @@ def tile_list_listed_slots_back_through_rest_pl_kernel(
                 wu_raw[32 * q : 32 * q + 4, 2 * K : 3 * K].bitcast(I32),
                 wu_scales[0, 4 * q : 4 * q + 4, :].bitcast(I32),
             )
-        wu_d = tile([P, PACK, 2 * P], U8, "wu_d")
-        wus_d = tile([P, PACK, P], U8, "wus_d")
-        nc.gpsimd.tensor_copy(
-            wu_d[:].rearrange("p t (m b) -> p t m b", b=2),
-            wu_raw[:, 0 : 2 * K].rearrange("p (m t b) -> p t m b", t=PACK, b=2),
-        )
-        nc.gpsimd.tensor_copy(wus_d[:], wu_raw[:, 2 * K : 3 * K].rearrange("p (m t) -> p t m", t=PACK))
 
-        for t in range(2, PACK):
+        for t in range(1, PACK):
             nc.vector.memset(pages[t][:], 0.0)
 
-        wd0 = tile([P, PASSES, P], I32, "wd0")
-        wds0 = tile([P, PASSES, P], U8, "wds0")
-        wdr = tile([P, PACK - 1, PASSES, P], I32, "wdr")
-        wdsr = tile([P, PACK - 1, PASSES, P], U8, "wdsr")
-        wd_v = wd_raw[:].rearrange("p z (m t) -> p z m t", t=PACK)
-        wds_v = wds_raw[:].rearrange("p z (m t) -> p z m t", t=PACK)
-        nc.vector.tensor_copy(wds0[:], wds_v[:, :, :, 0])
-        nc.vector.tensor_copy(wd0[:], wd_v[:, :, :, 0])
-        nc.vector.tensor_copy(wdr[:].rearrange("p t z m -> p z m t"), wd_v[:, :, :, 1:PACK])
-        nc.vector.tensor_copy(wdsr[:].rearrange("p t z m -> p z m t"), wds_v[:, :, :, 1:PACK])
+        wd_v = wd_raw[:].rearrange("p z (m t) -> p t z m", t=PACK)
+        wds_v = wds_raw[:].rearrange("p z (m t) -> p t z m", t=PACK)
+        wd_d, wds_d = [], []
+        for t, tags in ((0, ("late_c", "late_d")), (1, ("wd1", "late_g"))):
+            w = tile([P, PASSES, P], I32, "wd%d" % t, tags[0])
+            s = tile([P, PASSES, P], U8, "wds%d" % t, tags[1])
+            nc.vector.tensor_copy(w[:], wd_v[:, t, :, :])
+            nc.vector.tensor_copy(s[:], wds_v[:, t, :, :])
+            wd_d.append(w[:])
+            wds_d.append(s[:])
 
         def first_product(t, acc, lo, hi):
             for zp in range(PASSES):
-                w = wd0[:, zp, :] if t == 0 else wdr[:, t - 1, zp, :]
-                s = wds0[:, zp, :] if t == 0 else wdsr[:, t - 1, zp, :]
                 nc.tensor.matmul_mx(
                     out=acc,
-                    lhsT=w.bitcast(E4M3),
-                    lhsT_scale=s,
+                    lhsT=wd_d[t][:, zp, :].bitcast(E4M3),
+                    lhsT_scale=wds_d[t][:, zp, :],
                     rhs=g_w[:, zp, 2 * lo : 2 * hi].bitcast(E2M1),
                     rhs_scale=g_s[:, zp, lo:hi],
                     start=(zp == 0),
                     stop=(zp == PASSES - 1),
                 )
 
-        z_v = z.rearrange("(p t) j -> p t j", t=PACK)
-        z_a = tile([P, 2, J], F32, "z_a", "late_a")
-        z_b = tile([P, 2, J], F32, "z_b", "late_b")
-        nc.sync.dma_start(z_a[:], z_v[:, 0:2, :])
-        nc.sync.dma_start(z_b[:], z_v[:, 2:4, :])
-        z_rows = [z_a[:, 0, :], z_a[:, 1, :], z_b[:, 0, :], z_b[:, 1, :]]
-
         pairs = [tile([P, 2, 2 * HALF], BF16, "pairs%d" % h) for h in range(2)]
 
-        def multiply(engine, t, h):
-            cols = slice(h * HALF, (h + 1) * HALF)
-            gate = tile([P, HALF], F32, "gate%d_%d" % (t, h), "gate%d_%d" % (min(t, 2), h))
+        def gate_of(t, cols, tag):
+            gate = tile([P, cols.stop - cols.start], F32, "gate%d_%d" % (t, cols.start), tag)
             nc.scalar.activation(gate[:], z_rows[t][:, cols], RELU, scale=2.0)
-            engine.tensor_tensor(pairs[h][:, t // 2, t % 2 : 2 * HALF : 2], pages[t][:, cols], gate[:], MULT)
+            return gate
+
+        def multiply(engine, t, h, gate):
+            cols = slice(h * HALF, (h + 1) * HALF)
+            engine.tensor_tensor(pairs[h][:, t // 2, t % 2 : 2 * HALF : 2], pages[t][:, cols], gate, MULT)
 
         acc = bank(0, "d0a")
         first_product(0, acc[:, 0:FIRST], 0, FIRST)
@@ -134,34 +119,63 @@ def tile_list_listed_slots_back_through_rest_pl_kernel(
         acc = bank(1, "d0b")
         for lo in range(FIRST, I, FIRST):
             first_product(0, acc[:, lo - FIRST : lo], lo, lo + FIRST)
-        d0b = tile([P, I - FIRST], F32, "d0b_s", "late_f")
+        d0b = tile([P, I - FIRST], F32, "d0b_s")
         nc.scalar.copy(d0b[:], acc[:, 0 : I - FIRST])
         nc.vector.tensor_copy(pages[0][:].indirect(offsets[:, FIRST // 16 : I // 16]), d0b[:])
 
+        z_v = z.rearrange("(p t) j -> p t j", t=PACK)
+        z_0 = tile([P, J], F32, "z_0", "late_d")
+        z_1 = tile([P, J], F32, "z_1", "late_c")
+        nc.sync.dma_start(z_0[:], z_v[:, 0, :])
+        nc.sync.dma_start(z_1[:], z_v[:, 1, :])
+
         for t in range(1, PACK):
+            if t == 2:
+                z_b = tile([P, 2, J], F32, "z_b", "wd1")
+                nc.sync.dma_start(z_b[:], z_v[:, 2:4, :])
+                z_rows = [z_0[:], z_1[:], z_b[:, 0, :], z_b[:, 1, :]]
+                both = tile([P, 2, PASSES, 5 * P], U8, "wd23", "late_g")
+                w = both[:, :, :, 0 : 4 * P].bitcast(I32)
+                s = both[:, :, :, 4 * P : 5 * P]
+                nc.gpsimd.tensor_copy(s, wds_v[:, 2:PACK, :, :])
+                nc.gpsimd.tensor_copy(w, wd_v[:, 2:PACK, :, :])
+                wd_d.extend([w[:, 0, :, :], w[:, 1, :, :]])
+                wds_d.extend([s[:, 0, :, :], s[:, 1, :, :]])
             acc = bank(t + 1, "d%d" % t)
             first_product(t, acc[:], 0, I)
             d_s = tile([P, I], F32, "d%d_s" % t)
             nc.scalar.copy(d_s[:], acc[:])
             nc.vector.tensor_copy(pages[t][:].indirect(offsets[:]), d_s[:])
 
+        wu_d = tile([P, PACK, 3 * P], U8, "wu_d", "late_b")
+        nc.gpsimd.tensor_copy(
+            wu_d[:, :, 0 : 2 * P].rearrange("p t (m b) -> p t m b", b=2),
+            wu_raw[:, 0 : 2 * K].rearrange("p (m t b) -> p t m b", t=PACK, b=2),
+        )
+        nc.gpsimd.tensor_copy(wu_d[:, :, 2 * P : 3 * P], wu_raw[:, 2 * K : 3 * K].rearrange("p (m t) -> p t m", t=PACK))
+
         run_v = run.rearrange("(p t) j -> p t j", t=PACK)
-        runs = [tile([P, PACK, HALF], F32, "run%d" % h, ("late_e", "late_f")[h]) for h in range(2)]
+        runs = [tile([P, PACK, HALF], F32, "run%d" % h, ("late_a", "wu_raw")[h]) for h in range(2)]
         for h in range(2):
             nc.sync.dma_start(runs[h][:], run_v[:, :, h * HALF : (h + 1) * HALF])
 
-        for t in range(PACK - 1):
-            for h in range(2):
-                multiply(nc.gpsimd, t, h)
+        halves = [slice(h * HALF, (h + 1) * HALF) for h in range(2)]
         for h in range(2):
-            multiply(nc.vector, PACK - 1, h)
+            multiply(nc.gpsimd, 0, h, gate_of(0, halves[h], "gate0_%d" % h)[:])
+        gate = gate_of(1, slice(0, J), "late_g")
+        for h in range(2):
+            multiply(nc.gpsimd, 1, h, gate[:, halves[h]])
+        for t, engine in ((2, nc.gpsimd), (3, nc.vector)):
+            for h in range(2):
+                multiply(engine, t, h, gate_of(t, halves[h], ("late_h", "late_i")[h])[:])
 
         dz_w = [tile([P, HALF], I32, "dz_w%d" % h) for h in range(2)]
         dz_s = [tile([P, HALF], U8, "dz_s%d" % h) for h in range(2)]
         for q in range(4):
             h, lo = q // 2, (q % 2) * QUARTER
             grouped = tile([P, PACK * QUARTER], BF16, "dz_g%d" % q)
-            nc.scalar.copy(
+            weave = nc.vector.tensor_copy if q == 1 else nc.scalar.copy
+            weave(
                 grouped[:].bitcast(F32).rearrange("p (j u) -> p j u", u=2),
                 pairs[h][:].bitcast(F32)[:, :, lo : lo + QUARTER].rearrange("p u j -> p j u"),
             )
@@ -178,8 +192,8 @@ def tile_list_listed_slots_back_through_rest_pl_kernel(
             acc = bank((5 + PACK * h + t) % 8, "p%d_%d" % (h, t))
             nc.tensor.matmul_mx(
                 out=acc[:],
-                lhsT=wu_d[:, t, :].bitcast(E2M1),
-                lhsT_scale=wus_d[:, t, :],
+                lhsT=wu_d[:, t, 0 : 2 * P].bitcast(E2M1),
+                lhsT_scale=wu_d[:, t, 2 * P : 3 * P],
                 rhs=dz_w[h][:].bitcast(E5M2),
                 rhs_scale=dz_s[h][:],
                 start=True,
@@ -187,14 +201,10 @@ def tile_list_listed_slots_back_through_rest_pl_kernel(
             )
             return acc
 
-        def planes(q, y, on_gpsimd):
+        def planes(q, y):
             grouped = tile([P, QUARTER, PACK], BF16, "y_g%d" % q)
-            dst = grouped[:].rearrange("p (c i) t -> p c t i", i=4)
-            src = y.rearrange("p t (c i) -> p c t i", i=4)
-            if on_gpsimd:
-                nc.gpsimd.tensor_scalar(grouped[:], y.rearrange("p t j -> p j t"), 1.0, 0.0, MULT, ADD)
-            else:
-                nc.scalar.copy(dst, src)
+            copy = nc.vector.tensor_copy if q == 3 else nc.scalar.copy
+            copy(grouped[:].rearrange("p (c i) t -> p c t i", i=4), y.rearrange("p t (c i) -> p c t i", i=4))
             cols = slice(q * QUARTER, (q + 1) * QUARTER)
             nc.vector.quantize_mx(
                 out=y_w[:, cols].bitcast(E4M3), scales=y_s[:, cols], in_=grouped[:].rearrange("p j t -> p (j t)")
@@ -202,20 +212,16 @@ def tile_list_listed_slots_back_through_rest_pl_kernel(
             nc.sync.dma_start(words_v[:, cols], y_w[:, cols])
 
         accs = [[second_product(h, t) for t in range(PACK)] for h in range(2)]
-        y0 = tile([P, PACK, HALF], F32, "y0")
-        for t in range(PACK):
-            nc.vector.tensor_tensor(y0[:, t, :], accs[0][t][:], runs[0][:, t, :], ADD)
-            nc.sync.dma_start(out_v[:, t, 0:HALF], y0[:, t, :])
-        y1 = [tile([P, PACK, QUARTER], F32, "y1_%d" % e) for e in range(2)]
-        for e in range(2):
-            cols = slice(e * QUARTER, (e + 1) * QUARTER)
+        ys = [tile([P, PACK, HALF], F32, "y%d" % h) for h in range(2)]
+        for h in range(2):
             for t in range(PACK):
-                nc.vector.tensor_tensor(y1[e][:, t, :], accs[1][t][:, cols], runs[1][:, t, cols], ADD)
-            nc.sync.dma_start(out_v[:, :, HALF + e * QUARTER : HALF + (e + 1) * QUARTER], y1[e][:])
-        planes(0, y0[:, :, 0:QUARTER], False)
-        planes(1, y0[:, :, QUARTER:HALF], True)
-        planes(2, y1[0][:], False)
-        planes(3, y1[1][:], False)
+                last = h == 1 and t == PACK - 1
+                for lo, hi in ((0, QUARTER), (QUARTER, HALF)) if last else ((0, HALF),):
+                    nc.vector.tensor_tensor(ys[h][:, t, lo:hi], accs[h][t][:, lo:hi], runs[h][:, t, lo:hi], ADD)
+                nc.sync.dma_start(out_v[:, t, halves[h]], ys[h][:, t, :])
+        for q in range(4):
+            lo = (q % 2) * QUARTER
+            planes(q, ys[q // 2][:, :, lo : lo + QUARTER])
         for q in range(4):
             queue = nc.sync if q % 2 == 0 else nc.scalar
             queue.dma_start(out_2[0, 4 * q : 4 * q + 4, :].bitcast(I32), y_s[32 * q : 32 * q + 4, :].bitcast(I32))

@@ -42,8 +42,8 @@ def tile_list_listed_slots_back_through_rest_pl_kernel(
         offsets = tile([P, I // 16], U16, "offsets")
         wd_raw = tile([P, PASSES, R], I32, "wd_raw", "late_b")
         wds_raw = tile([P, PASSES, R], U8, "wds_raw", "late_a")
-        g_w = tile([P, PASSES, 2 * I], U8, "g_w", "late_h")
-        g_s = tile([P, PASSES, I], U8, "g_s", "late_i")
+        g_w = tile([P, PASSES, 2 * I], U8, "g_w")
+        g_s = tile([P, PASSES, I], U8, "g_s")
 
         nc.vector.memset(wds_raw[:].bitcast(I32), 0)
 
@@ -77,16 +77,18 @@ def tile_list_listed_slots_back_through_rest_pl_kernel(
         for t in range(1, PACK):
             nc.vector.memset(pages[t][:], 0.0)
 
-        wd_v = wd_raw[:].rearrange("p z (m t) -> p t z m", t=PACK)
-        wds_v = wds_raw[:].rearrange("p z (m t) -> p t z m", t=PACK)
-        wd_d, wds_d = [], []
-        for t, tags in ((0, ("late_c", "late_d")), (1, ("wd1", "late_g"))):
-            w = tile([P, PASSES, P], I32, "wd%d" % t, tags[0])
-            s = tile([P, PASSES, P], U8, "wds%d" % t, tags[1])
-            nc.vector.tensor_copy(w[:], wd_v[:, t, :, :])
-            nc.vector.tensor_copy(s[:], wds_v[:, t, :, :])
-            wd_d.append(w[:])
-            wds_d.append(s[:])
+        wd_v = wd_raw[:].rearrange("p z (m t) -> p z m t", t=PACK)
+        wds_v = wds_raw[:].rearrange("p z (m t) -> p z m t", t=PACK)
+        wd0 = tile([P, PASSES, P], I32, "wd0", "late_c")
+        wds0 = tile([P, PASSES, P], U8, "wds0", "late_d")
+        wdr = tile([P, PACK - 1, PASSES, P], I32, "wdr", "late_g")
+        wdsr = tile([P, PACK - 1, PASSES, P], U8, "wdsr")
+        nc.vector.tensor_copy(wd0[:], wd_v[:, :, :, 0])
+        nc.vector.tensor_copy(wds0[:], wds_v[:, :, :, 0])
+        nc.vector.tensor_copy(wdr[:].rearrange("p t z m -> p z m t"), wd_v[:, :, :, 1:PACK])
+        nc.vector.tensor_copy(wdsr[:].rearrange("p t z m -> p z m t"), wds_v[:, :, :, 1:PACK])
+        wd_d = [wd0[:]] + [wdr[:, t, :, :] for t in range(PACK - 1)]
+        wds_d = [wds0[:]] + [wdsr[:, t, :, :] for t in range(PACK - 1)]
 
         def first_product(t, acc, lo, hi):
             for zp in range(PASSES):
@@ -130,44 +132,37 @@ def tile_list_listed_slots_back_through_rest_pl_kernel(
         nc.sync.dma_start(z_1[:], z_v[:, 1, :])
 
         for t in range(1, PACK):
-            if t == 2:
-                z_b = tile([P, 2, J], F32, "z_b", "wd1")
-                nc.sync.dma_start(z_b[:], z_v[:, 2:4, :])
-                z_rows = [z_0[:], z_1[:], z_b[:, 0, :], z_b[:, 1, :]]
-                both = tile([P, 2, PASSES, 5 * P], U8, "wd23", "late_g")
-                w = both[:, :, :, 0 : 4 * P].bitcast(I32)
-                s = both[:, :, :, 4 * P : 5 * P]
-                nc.gpsimd.tensor_copy(s, wds_v[:, 2:PACK, :, :])
-                nc.gpsimd.tensor_copy(w, wd_v[:, 2:PACK, :, :])
-                wd_d.extend([w[:, 0, :, :], w[:, 1, :, :]])
-                wds_d.extend([s[:, 0, :, :], s[:, 1, :, :]])
             acc = bank(t + 1, "d%d" % t)
             first_product(t, acc[:], 0, I)
             d_s = tile([P, I], F32, "d%d_s" % t)
             nc.scalar.copy(d_s[:], acc[:])
             nc.vector.tensor_copy(pages[t][:].indirect(offsets[:]), d_s[:])
 
-        wu_d = tile([P, PACK, 3 * P], U8, "wu_d", "late_b")
+        z_b = tile([P, 2, J], F32, "z_b", "late_g")
+        nc.sync.dma_start(z_b[:], z_v[:, 2:4, :])
+        z_rows = [z_0[:], z_1[:], z_b[:, 0, :], z_b[:, 1, :]]
+
+        wu_d = tile([P, PACK, 3 * P], U8, "wu_d", "late_a")
         nc.gpsimd.tensor_copy(
             wu_d[:, :, 0 : 2 * P].rearrange("p t (m b) -> p t m b", b=2),
             wu_raw[:, 0 : 2 * K].rearrange("p (m t b) -> p t m b", t=PACK, b=2),
         )
         nc.gpsimd.tensor_copy(wu_d[:, :, 2 * P : 3 * P], wu_raw[:, 2 * K : 3 * K].rearrange("p (m t) -> p t m", t=PACK))
 
-        run_v = run.rearrange("(p t) j -> p t j", t=PACK)
-        runs = [tile([P, PACK, HALF], F32, "run%d" % h, ("late_a", "wu_raw")[h]) for h in range(2)]
-        for h in range(2):
-            nc.sync.dma_start(runs[h][:], run_v[:, :, h * HALF : (h + 1) * HALF])
-
         halves = [slice(h * HALF, (h + 1) * HALF) for h in range(2)]
         for h in range(2):
             multiply(nc.gpsimd, 0, h, gate_of(0, halves[h], "gate0_%d" % h)[:])
-        gate = gate_of(1, slice(0, J), "late_g")
+        gate = gate_of(1, slice(0, J), "gate1")
         for h in range(2):
             multiply(nc.gpsimd, 1, h, gate[:, halves[h]])
+        run_v = run.rearrange("(p t) j -> p t j", t=PACK)
+        runs = [tile([P, PACK, HALF], F32, "run%d" % h, ("late_d", "late_c")[h]) for h in range(2)]
+        for h in range(2):
+            nc.sync.dma_start(runs[h][:], run_v[:, :, h * HALF : (h + 1) * HALF])
+
         for t, engine in ((2, nc.gpsimd), (3, nc.vector)):
             for h in range(2):
-                multiply(engine, t, h, gate_of(t, halves[h], ("late_h", "late_i")[h])[:])
+                multiply(engine, t, h, gate_of(t, halves[h], "gate0_%d" % h)[:])
 
         dz_w = [tile([P, HALF], I32, "dz_w%d" % h) for h in range(2)]
         dz_s = [tile([P, HALF], U8, "dz_s%d" % h) for h in range(2)]

from contextlib import ExitStack

import concourse.mybir as mybir

N, R, K, J, I = 1024, 512, 512, 1024, 512
FLOPS = 2 * N * R * I + 2 * R * K * J

F32 = mybir.dt.float32
BF16 = mybir.dt.bfloat16
I32 = mybir.dt.int32
U16 = mybir.dt.uint16
U8 = mybir.dt.uint8
E4M3 = mybir.dt.float8_e4m3fn_x4
E5M2 = mybir.dt.float8_e5m2_x4
E2M1 = mybir.dt.float4_e2m1fn_x4
MULT = mybir.AluOpType.mult
ADD = mybir.AluOpType.add
RELU = mybir.ActivationFunctionType.Relu

P = 128
PACK = 4
PASSES = N // (P * PACK)
HALF = 512
QUARTER = 256
FIRST = 128


def tile_list_listed_slots_back_through_rest_pl_kernel(
    tc, g_words, g_scales, wd_words, wd_scales, z, wu_words, wu_scales, run, offs, out_0, out_1, out_2
):
    nc = tc.nc
    with ExitStack() as ctx:
        sb = ctx.enter_context(tc.tile_pool(name="sb", bufs=1))
        ps = ctx.enter_context(tc.psum_pool(name="ps", bufs=1))

        def tile(shape, dtype, name, tag=None):
            return sb.tile(shape, dtype, name=name, tag=tag or name, align_bytes=64)

        def bank(b, name):
            return ps.tile([P, HALF], F32, name=name, tag="bank%d" % b)

        offsets = tile([P, I // 16], U16, "offsets")
        wd_raw = tile([P, PASSES, R], I32, "wd_raw", "late_b")
        wds_raw = tile([P, PASSES, R], U8, "wds_raw", "late_a")
        g_w = tile([P, PASSES, 2 * I], U8, "g_w")
        g_s = tile([P, PASSES, I], U8, "g_s")

        nc.vector.memset(wds_raw[:].bitcast(I32), 0)

        queues = (nc.sync, nc.scalar)
        for q in range(4):
            queues[q % 2].dma_start(
                g_s[32 * q : 32 * q + 4, :, :].bitcast(I32),
                g_scales[:, 4 * q : 4 * q + 4, :].rearrange("z q c -> q z c").bitcast(I32),
            )
        nc.sync.dma_start(wd_raw[:], wd_words.rearrange("z p c r -> p z (c r)").bitcast(I32))
        nc.scalar.dma_start(g_w[:].bitcast(I32), g_words.rearrange("z p b -> p z b").bitcast(I32))
        for q in range(4):
            queues[q % 2].dma_start(
                wds_raw[32 * q : 32 * q + 4, :, :].bitcast(I32),
                wd_scales[:, 4 * q : 4 * q + 4, :].rearrange("z q c -> q z c").bitcast(I32),
            )
        nc.sync.dma_start(offsets[:], offs)

        pages = [tile([P, J], F32, "page%d" % t) for t in range(PACK)]
        nc.vector.memset(pages[0][:], 0.0)

        wu_raw = tile([P, 3 * K], U8, "wu_raw")
        nc.vector.memset(wu_raw[:].bitcast(I32), 0)
        nc.sync.dma_start(wu_raw[:, 0 : 2 * K].bitcast(I32), wu_words[0].bitcast(I32))
        for q in range(4):
            nc.sync.dma_start(
                wu_raw[32 * q : 32 * q + 4, 2 * K : 3 * K].bitcast(I32),
                wu_scales[0, 4 * q : 4 * q + 4, :].bitcast(I32),
            )

        for t in range(1, PACK):
            nc.vector.memset(pages[t][:], 0.0)

        wd_v = wd_raw[:].rearrange("p z (m t) -> p z m t", t=PACK)
        wds_v = wds_raw[:].rearrange("p z (m t) -> p z m t", t=PACK)
        wd0 = tile([P, PASSES, P], I32, "wd0", "late_c")
        wds0 = tile([P, PASSES, P], U8, "wds0", "late_d")
        wdr = tile([P, PACK - 1, PASSES, P], I32, "wdr", "late_g")
        wdsr = tile([P, PACK - 1, PASSES, P], U8, "wdsr")
        nc.vector.tensor_copy(wd0[:], wd_v[:, :, :, 0])
        nc.vector.tensor_copy(wds0[:], wds_v[:, :, :, 0])
        nc.vector.tensor_copy(wdr[:].rearrange("p t z m -> p z m t"), wd_v[:, :, :, 1:PACK])
        nc.vector.tensor_copy(wdsr[:].rearrange("p t z m -> p z m t"), wds_v[:, :, :, 1:PACK])
        wd_d = [wd0[:]] + [wdr[:, t, :, :] for t in range(PACK - 1)]
        wds_d = [wds0[:]] + [wdsr[:, t, :, :] for t in range(PACK - 1)]

        def first_product(t, acc, lo, hi):
            for zp in range(PASSES):
                nc.tensor.matmul_mx(
                    out=acc,
                    lhsT=wd_d[t][:, zp, :].bitcast(E4M3),
                    lhsT_scale=wds_d[t][:, zp, :],
                    rhs=g_w[:, zp, 2 * lo : 2 * hi].bitcast(E2M1),
                    rhs_scale=g_s[:, zp, lo:hi],
                    start=(zp == 0),
                    stop=(zp == PASSES - 1),
                )

        pairs = [tile([P, 2, 2 * HALF], BF16, "pairs%d" % h) for h in range(2)]

        def gate_of(t, cols, tag):
            gate = tile([P, cols.stop - cols.start], F32, "gate%d_%d" % (t, cols.start), tag)
            nc.scalar.activation(gate[:], z_rows[t][:, cols], RELU, scale=2.0)
            return gate

        def multiply(engine, t, h, gate):
            cols = slice(h * HALF, (h + 1) * HALF)
            engine.tensor_tensor(pairs[h][:, t // 2, t % 2 : 2 * HALF : 2], pages[t][:, cols], gate, MULT)

        acc = bank(0, "d0a")
        first_product(0, acc[:, 0:FIRST], 0, FIRST)
        d0a = tile([P, FIRST], F32, "d0a_s", "late_e")
        nc.scalar.copy(d0a[:], acc[:, 0:FIRST])
        nc.vector.tensor_copy(pages[0][:].indirect(offsets[:, 0 : FIRST // 16]), d0a[:])
        acc = bank(1, "d0b")
        for lo in range(FIRST, I, FIRST):
            first_product(0, acc[:, lo - FIRST : lo], lo, lo + FIRST)
        d0b = tile([P, I - FIRST], F32, "d0b_s")
        nc.scalar.copy(d0b[:], acc[:, 0 : I - FIRST])
        nc.vector.tensor_copy(pages[0][:].indirect(offsets[:, FIRST // 16 : I // 16]), d0b[:])

        z_v = z.rearrange("(p t) j -> p t j", t=PACK)
        z_0 = tile([P, J], F32, "z_0", "late_d")
        z_1 = tile([P, J], F32, "z_1", "late_c")
        nc.sync.dma_start(z_0[:], z_v[:, 0, :])
        nc.sync.dma_start(z_1[:], z_v[:, 1, :])

        for t in range(1, PACK):
            acc = bank(t + 1, "d%d" % t)
            first_product(t, acc[:], 0, I)
            d_s = tile([P, I], F32, "d%d_s" % t)
            nc.scalar.copy(d_s[:], acc[:])
            nc.vector.tensor_copy(pages[t][:].indirect(offsets[:]), d_s[:])

        z_b = tile([P, 2, J], F32, "z_b", "late_g")
        nc.sync.dma_start(z_b[:], z_v[:, 2:4, :])
        z_rows = [z_0[:], z_1[:], z_b[:, 0, :], z_b[:, 1, :]]

        wu_d = tile([P, PACK, 3 * P], U8, "wu_d", "late_a")
        nc.gpsimd.tensor_copy(
            wu_d[:, :, 0 : 2 * P].rearrange("p t (m b) -> p t m b", b=2),
            wu_raw[:, 0 : 2 * K].rearrange("p (m t b) -> p t m b", t=PACK, b=2),
        )
        nc.gpsimd.tensor_copy(wu_d[:, :, 2 * P : 3 * P], wu_raw[:, 2 * K : 3 * K].rearrange("p (m t) -> p t m", t=PACK))

        halves = [slice(h * HALF, (h + 1) * HALF) for h in range(2)]
        for h in range(2):
            multiply(nc.gpsimd, 0, h, gate_of(0, halves[h], "gate0_%d" % h)[:])
        gate = gate_of(1, slice(0, J), "gate1")
        for h in range(2):
            multiply(nc.gpsimd, 1, h, gate[:, halves[h]])
        run_v = run.rearrange("(p t) j -> p t j", t=PACK)
        runs = [tile([P, PACK, HALF], F32, "run%d" % h, ("late_d", "late_c")[h]) for h in range(2)]
        for h in range(2):
            nc.sync.dma_start(runs[h][:], run_v[:, :, h * HALF : (h + 1) * HALF])

        for t, engine in ((2, nc.gpsimd), (3, nc.vector)):
            for h in range(2):
                multiply(engine, t, h, gate_of(t, halves[h], "gate0_%d" % h)[:])

        dz_w = [tile([P, HALF], I32, "dz_w%d" % h) for h in range(2)]
        dz_s = [tile([P, HALF], U8, "dz_s%d" % h) for h in range(2)]
        for q in range(4):
            h, lo = q // 2, (q % 2) * QUARTER
            grouped = tile([P, PACK * QUARTER], BF16, "dz_g%d" % q)
            weave = nc.vector.tensor_copy if q == 1 else nc.scalar.copy
            weave(
                grouped[:].bitcast(F32).rearrange("p (j u) -> p j u", u=2),
                pairs[h][:].bitcast(F32)[:, :, lo : lo + QUARTER].rearrange("p u j -> p j u"),
            )
            nc.vector.quantize_mx(
                out=dz_w[h][:, lo : lo + QUARTER].bitcast(E5M2), scales=dz_s[h][:, lo : lo + QUARTER], in_=grouped[:]
            )

        out_v = out_0.rearrange("(p t) j -> p t j", t=PACK)
        words_v = out_1[0].rearrange("p c r -> p (c r)").bitcast(I32)
        y_w = tile([P, J], I32, "y_w")
        y_s = tile([P, J], U8, "y_s")

        def second_product(h, t):
            acc = bank((5 + PACK * h + t) % 8, "p%d_%d" % (h, t))
            nc.tensor.matmul_mx(
                out=acc[:],
                lhsT=wu_d[:, t, 0 : 2 * P].bitcast(E2M1),
                lhsT_scale=wu_d[:, t, 2 * P : 3 * P],
                rhs=dz_w[h][:].bitcast(E5M2),
                rhs_scale=dz_s[h][:],
                start=True,
                stop=True,
            )
            return acc

        def planes(q, y):
            grouped = tile([P, QUARTER, PACK], BF16, "y_g%d" % q)
            copy = nc.vector.tensor_copy if q == 3 else nc.scalar.copy
            copy(grouped[:].rearrange("p (c i) t -> p c t i", i=4), y.rearrange("p t (c i) -> p c t i", i=4))
            cols = slice(q * QUARTER, (q + 1) * QUARTER)
            nc.vector.quantize_mx(
                out=y_w[:, cols].bitcast(E4M3), scales=y_s[:, cols], in_=grouped[:].rearrange("p j t -> p (j t)")
            )
            nc.sync.dma_start(words_v[:, cols], y_w[:, cols])

        accs = [[second_product(h, t) for t in range(PACK)] for h in range(2)]
        ys = [tile([P, PACK, HALF], F32, "y%d" % h) for h in range(2)]
        for h in range(2):
            for t in range(PACK):
                last = h == 1 and t == PACK - 1
                for lo, hi in ((0, QUARTER), (QUARTER, HALF)) if last else ((0, HALF),):
                    nc.vector.tensor_tensor(ys[h][:, t, lo:hi], accs[h][t][:, lo:hi], runs[h][:, t, lo:hi], ADD)
                nc.sync.dma_start(out_v[:, t, halves[h]], ys[h][:, t, :])
        for q in range(4):
            lo = (q % 2) * QUARTER
            planes(q, ys[q // 2][:, :, lo : lo + QUARTER])
        for q in range(4):
            queue = nc.sync if q % 2 == 0 else nc.scalar
            queue.dma_start(out_2[0, 4 * q : 4 * q + 4, :].bitcast(I32), y_s[32 * q : 32 * q + 4, :].bitcast(I32))
